import numpy as np, ml_dtypes
CORES = [36,164,52,180,100,228,116,244]
N = 8
import mx_ref
BF = ml_dtypes.bfloat16
def pick(q, e):
    c = np.concatenate([q[0].reshape(128, -1, 4), np.zeros((128, 1, 4), np.uint8)], axis=1); s = np.concatenate([q[1], np.ones((16, 1), np.uint8)], axis=1)
    return (np.ascontiguousarray(c[:, e].reshape(128, -1)), np.ascontiguousarray(s[:, e]))
def join(*qs):
    return (np.concatenate([q[0] for q in qs], axis=1), np.concatenate([q[1] for q in qs], axis=1))
def put(q, e, v):
    c, s = q[0].reshape(128, -1, 4).copy(), q[1].copy(); c[:, e] = v[0].reshape(128, -1, 4); s[:, e] = v[1]
    return (c.reshape(128, -1), s)
def pk(c, s):
    return (np.ascontiguousarray(c), mx_ref.live(s))
def emit(q):
    return q[0], q[1]
def cols(t, e):
    v = np.concatenate([t.reshape(128, -1, 4), np.zeros((128, 1, 4), BF)], axis=1)
    return np.ascontiguousarray(v[:, e]).reshape(128, -1)
def cut(t, i, w=512):
    return t[:, w * i:w * i + w]
def decode(q):
    o = []
    for b in range(4):
        e = np.zeros((128, 128, 4), np.float32); e[np.arange(128), np.arange(128), b] = 1
        o.append(mx_ref.matmul(mx_ref.quantize(e.reshape(128, 512).astype(BF)), q))
    return np.stack(o, axis=2).reshape(128, -1)
def f(rng, *shape):
    return mx_ref.flush((rng.standard_normal(shape, dtype=np.float32) * np.exp2(rng.integers(-2, 3, shape[:-1] + (1,)))).astype(BF))
def wide(rng, *shape, cols=0):
    v = rng.standard_normal(shape, dtype=np.float32) * np.exp2(rng.integers(-12, 13, shape)).astype(np.float32)
    if cols: v *= np.repeat(np.exp2(rng.integers(-cols, cols + 1, shape[:-2] + (1, shape[-1] // 4))) * (rng.random(shape[:-2] + (1, shape[-1] // 4)) > 0.0625), 4, axis=-1).astype(np.float32)
    return mx_ref.flush(v.astype(BF))
G, T, CAPP, R = 16, 96, 32, 2
def fit(v):
    v = np.array(v, np.float32)
    v[np.abs(v) < np.float32(2.0 ** -10)] = 0
    return v.astype(BF)
def plain(rng):
    return {"cb": fit(f(rng, N, 128, 4 * G)), "x": fit(f(rng, N, 128, 4 * R * T)), "w": f(rng, N, 128, 512)}
def part(rng, lab, k):
    s = (128, len(k), 4)
    v = np.where(k[None, :, None] == 2, rng.standard_normal(s), 1 + rng.random(s))
    return (v * (lab[:, None] == k[None, :])[:, :, None]).reshape(128, -1)
def setup_inputs(rng):
    return plain(rng)
def setup_inputs_crowd(rng):
    d = plain(rng)
    lab = rng.permutation(np.repeat([0, 1, 2], [40, 40, 48]))
    q, g = int(rng.integers(0, N - 2)), rng.permutation(G)[:2]
    home = int(rng.integers(0, R))
    rush = (home + 1 + int(rng.integers(0, R - 1))) % R
    cb = np.stack([part(rng, lab, np.full(G, 2)) for r in range(N)])
    k, size = np.zeros(G, int), np.full(G, 2.0 ** -6)
    k[g[1]] = 1
    size[g] = 1
    cb[q] = part(rng, lab, k) * np.repeat(size, 4)
    kinds = np.full((N, R, T), 2)
    for t in range(R):
        three, whole = np.sort(rng.permutation(N)[:3]), -1
        if t == home: three = np.concatenate([[q], np.sort(q + 1 + rng.permutation(N - 1 - q)[:2])])
        if t == rush:
            four, j = np.sort(rng.permutation(N)[:4]), int(rng.integers(0, 3))
            three, whole = np.delete(four, j), int(four[j])
        for s in range(N):
            more = int(rng.integers(1, T // 8 + 1))
            if s == three[0]: e = np.concatenate([np.zeros(CAPP, int), np.ones(more, int)])
            elif s == three[1]: e = np.concatenate([np.zeros(CAPP - 1, int), np.ones(1, int)])
            elif s == three[2]: e = np.concatenate([np.zeros(CAPP - 1, int), np.ones(1, int), rng.integers(0, 2, more)])
            elif s == whole: e = np.concatenate([np.zeros(CAPP, int), np.ones(T - CAPP, int)])
            else: e = np.zeros(int(rng.integers(CAPP // 2, CAPP + T // 8 + 1)), int)
            kinds[s, t, np.sort(rng.permutation(T)[:len(e)])] = e
    d["cb"], d["x"] = fit(cb), fit(np.stack([part(rng, lab, kinds[s].reshape(-1)) for s in range(N)]))
    return d
def setup_inputs_ties(rng):
    d = plain(rng)
    H = G // 2
    shared = fit(rng.standard_normal((128, 4 * H)))
    for r in range(N):
        both = np.concatenate([shared, fit(rng.standard_normal((128, 4 * H)))], axis=1)
        d["cb"][r] = cols(both, rng.permutation(np.concatenate([rng.integers(0, H, G - H), H + np.arange(H)])))
        v = cut(d["x"][r], 0, 4 * T).copy().reshape(128, T, 4)
        at = rng.permutation(T)
        v[:, at[:H]] = shared.reshape(128, H, 4)
        v[:, at[H:H + T // 16]] = 0
        d["x"][r] = np.concatenate([cols(v.reshape(128, -1), rng.permutation(T)) for t in range(R)], axis=1)
    return d
def setup_inputs_full(rng):
    d = plain(rng)
    at = rng.permutation(128)
    own = at[None, :] == np.arange(128)[:, None]
    cb = (1 + rng.random((128, 128, 4))) * np.where(own, 1.0, 2.0 ** -8)[:, :, None]
    kinds, who = np.zeros((N, R, T), int), np.arange(128) // G
    least, below = [], []
    for t in range(R):
        s, q = [int(v) for v in rng.permutation(N)[:2]]
        mine, free = np.flatnonzero(who == q), np.flatnonzero(who != q)
        if t == 0 or t == R - 1:
            least.append(int(rng.choice([v for v in free if G <= v < 128 - G and v not in least])))
            free = free[free != least[-1]]
            below.append((s + 1 + int(rng.integers(0, N - 1))) % N)
        for r in range(N):
            if r == s: kinds[r, t] = rng.permutation(np.concatenate([mine, mine, rng.choice(free, T - 2 * G)]))
            elif r < s: kinds[r, t] = rng.choice(free, T)
            else: kinds[r, t] = rng.choice(np.concatenate([free, mine]), T)
    x = np.zeros((N, 128, R * T, 4))
    for r in range(N):
        k = kinds[r].reshape(-1)
        x[r] = np.where(own[:, k][:, :, None], 1 + rng.random((128, R * T, 4)), (2 * rng.random((128, R * T, 4)) - 1) * 2.0 ** -7)
    x[below[0]][:, :2] = -(1 + rng.random((128, 2, 4))) * np.where(own[:, least[0]], 2.0 ** -9, 2.0 ** -6)[:, None, None]
    size = np.where(own[:, least[1]], 2.0 ** 15, np.where(own[:, least[0]], 2.0 ** 24, 2.0 ** 21))
    i = (R - 1) * T
    x[below[1]][:, i:i + 2] = -(3 + rng.random((128, 2, 4))) * size[:, None, None]
    d["cb"] = fit(np.stack([cb[:, G * r:G * r + G].reshape(128, -1) for r in range(N)]))
    d["x"] = fit(x.reshape(N, 128, -1))
    return d
def setup_inputs_idle(rng):
    d = plain(rng)
    q, own = int(rng.integers(0, N)), rng.permutation(128) < 64
    cb = rng.standard_normal((N, 128, 4 * G))
    for r in range(N): cb[r] *= (own if r == q else ~own)[:, None]
    early = np.arange(4 * R * T) < 4 * (R - 1) * T
    d["cb"], d["x"] = fit(cb), fit(d["x"].astype(np.float32) * ~(own[:, None] & early[None, :]))
    return d
def setup_inputs_spread(rng):
    d = plain(rng)
    d["cb"] = fit(wide(rng, N, 128, 4 * G).astype(np.float32) * 64)
    d["x"] = fit(wide(rng, N, 128, 4 * R * T, cols=4).astype(np.float32) * 64)
    return d
def check_inputs(d):
    b = []
    for k, lo, hi in (("cb", -10, 28), ("x", -10, 28), ("w", -30, 30)):
        v = np.abs(d[k].astype(np.float32))
        if not (np.isfinite(v).all() and ((v == 0) | (v >= 2.0 ** lo) & (v <= 2.0 ** hi)).all()): b.append("a value of " + k)
    return b
def admitted(win):
    a = np.full((2, 128), -1)
    for s in range(N):
        n = np.zeros(N, int)
        for i in range(T):
            k = win[T * s + i]
            n[k // G] += 1
            if n[k // G] > CAPP: continue
            if a[0, k] < 0: a[0, k] = T * s + i
            elif a[1, k] < 0: a[1, k] = T * s + i
    return a
def reference(cb, x, w):
    y, ids = np.zeros((N, 128, R * 2 * G), np.float32), np.zeros((N, 1, R * 2 * G), np.float32)
    oc, osc = np.zeros((N, 128, 4 * G), np.uint8), np.zeros((N, 16, G), np.uint8)
    half, quarter = np.float32(0.5), np.float32(0.25)
    qw = [mx_ref.quantize(np.ascontiguousarray(w[r])) for r in range(N)]
    c = join(*[mx_ref.quantize(np.ascontiguousarray(cb[r])) for r in range(N)])
    for t in range(R):
        tok = join(*[mx_ref.quantize(np.ascontiguousarray(cut(x[s], t, 4 * T))) for s in range(N)])
        a = admitted(np.argmax(mx_ref.matmul(c, tok) + np.float32(0), axis=0))
        for r in range(N):
            e = a[:, G * r:G * r + G].T.reshape(-1)
            i = t * 2 * G
            y[r, :, i:i + 2 * G] = mx_ref.matmul(qw[r], pick(tok, e))
            ids[r, 0, i:i + 2 * G] = e
        v = decode(join(c, pick(tok, a[0]), pick(tok, a[1]))).reshape(128, 3, 128, 4)
        one = half * v[:, 0] + half * v[:, 1]
        two = half * v[:, 0] + (quarter * v[:, 1] + quarter * v[:, 2])
        new = np.where((a[1] >= 0)[None, :, None], two, one).reshape(128, 512).astype(BF)
        moved = np.flatnonzero(a[0] >= 0)
        c = put(c, moved, pick(mx_ref.quantize(np.ascontiguousarray(new)), moved))
    for r in range(N):
        oc[r], osc[r] = emit(pick(c, np.arange(G * r, G * r + G)))
    return {"y": y, "ids": ids, "oc": oc, "osc": osc}

@@ -1,0 +1,316 @@
+from concourse.bass import DstId, RemoteDMATransfer
+from concourse.mybir import dt, AluOpType as Op, AxisListType, ActivationFunctionType as Act
+
+N, G, TOK, CAPP, R = 8, 16, 96, 32, 2
+K = N * G
+C2 = 2 * G
+LW = N * C2
+
+_F, _B, _U, _Q, _S = "float32", "bfloat16", "uint16", "float8_e4m3fn_x4", "uint8"
+SCRATCH = {}
+
+
+def _buf(name, n, d):
+    SCRATCH[name] = ("sbuf", [128, n], d)
+
+
+def _mx(name, n):
+    _buf(name + "c", n, _Q)
+    _buf(name + "s", n, _S)
+
+
+for _n, _w in (("cbt", 512), ("xt", 896), ("wt", 512), ("zt", 512), ("ub", 512), ("ab", 2048), ("ob", 512),
+               ("eb", 2048), ("hb", 544), ("fb", 516), ("nt", 512)):
+    _buf(_n, _w, _B)
+for _n, _w in (("xq", 224), ("wq", 128), ("uq", 128), ("aq", 512), ("oq", 128), ("eq", 512), ("hq", 136), ("fa", 192),
+               ("fo", 192), ("cw0", 144), ("cw1", 144), ("cw2", 16), ("call0", 128), ("call1", 128), ("slot0", 256),
+               ("slot1", 256), ("land0", 384), ("land1", 384), ("pick", 144)):
+    _mx(_n, _w)
+for _n, _w in (("jj", 128), ("zf", 128), ("cm", 128), ("lm", 8), ("vd", 16), ("vz", 16), ("gcol", 1), ("rst", 48), ("rv", 16),
+               ("cum", 16), ("lt", 48), ("sc", 48), ("thr", 1), ("mv", 1), ("lf", 16), ("idb", 16), ("num", 16), ("numv", 16),
+               ("eq1", 16), ("eq2", 16), ("id1", 16), ("id2", 16), ("idr", 2), ("idt0", 2), ("idt1", 2), ("dc0", 64), ("dc1", 64),
+               ("ysb", 64)):
+    _buf(_n, _w, _F)
+for _n, _w in (("v0", 16), ("v1", 16), ("lists0", 16), ("lists1", 16), ("po", 4), ("fin", 2), ("own16", 2)):
+    _buf(_n, _w, _U)
+_buf("pi", 1, "int32")
+_buf("pg", 1, "int32")
+for _n, _w in (("pss", 512), ("psp", 512), ("psl", 512), ("psf", 512), ("psn", 2048)):
+    SCRATCH[_n] = ("psum", [128, _w], _F)
+
+SEMAPHORES = ["ldc", "ldx", "ldw", "io", "dv", "z", "eb", "q0", "qx", "qw", "qk", "own", "arrc0", "arrc1", "arrl0", "arrl1",
+              "arrt0", "arrt1", "sent", "s", "cm", "h", "hq", "pc", "fa", "fo", "lim", "fs", "v", "pk", "pks", "ol", "pp",
+              "n0", "n1", "n2", "n3", "y", "yc", "wn", "cn", "cns", "dd", "dc", "id", "out", "outs"]
+
+
+def rank_program(g, core, T, topo):
+    r = T.rank_of(core)
+    if r is None:
+        return
+    ve, ac, te, sy = g.vector, g.scalar, g.tensor, g.sync
+    count, seen = {}, {}
+
+    def inc(call, name, n=1):
+        call.then_inc(T.sem[name], n)
+        count[name] = count.get(name, 0) + n
+
+    def wait(queue, *names):
+        for name in names:
+            queue.wait_ge(T.sem[name], count[name])
+            seen[name] = count[name]
+
+    def cc(name, a, b):
+        return T[name + "c"][:, a:b].bitcast(dt.uint8)
+
+    def sc(name, a, b):
+        return T[name + "s"][:, a:b]
+
+    def quant(name, a, b, tile):
+        return ve.quantize_mx(T[name + "c"][:, a:b], T[name + "s"][:, a:b], tile)
+
+    def mm(out, w, wa, x, xa, xb, start=True, stop=True):
+        return te.matmul_mx(out, T[w + "c"][:, wa:wa + 128], T[w + "s"][:, wa:wa + 128], T[x + "c"][:, xa:xb],
+                            T[x + "s"][:, xa:xb], start, stop)
+
+    def pickc(dst, a, b, src, c, d, offs):
+        return ve.tensor_copy(T[dst + "c"][:, a:b].bitcast(dt.uint32), T[src + "c"][:, c:d].bitcast(dt.uint32).indirect(offs))
+
+    def picks(dst, a, b, src, c, d, offs):
+        return ac.activation(T[dst + "s"][:, a:b], T[src + "s"][:, c:d].indirect(offs), Act.Copy)
+
+    others = [d for d in range(N) if d != r]
+    dest = {}
+    for d in others:
+        rid, pid = topo.addr(T.cores[d], core)
+        dest[d] = DstId(rid=rid, pnc=pid)
+    engs = {d: topo.engines(core, T.cores[d]) for d in others}
+
+    def to_all(view, sem):
+        g.remote_dma_fused([RemoteDMATransfer(dst_ids=[dest[d] for d in others], dma_engine_mask=topo.mask(core, T.cores[others[0]]),
+                                              remote_sem=T.sem[sem], srcs=[view[0]], dsts=[view[1]] * len(others))],
+                           local_sem=T.sem.sent)
+        count["sent"] = count.get("sent", 0) + len(engs[others[0]])
+
+    def to_each(src, dst, sem):
+        g.remote_dma_fused([RemoteDMATransfer(dst_ids=[dest[d]], dma_engine_mask=1 << engs[d][i], remote_sem=T.sem[sem],
+                                              srcs=[src(d)], dsts=[dst]) for i, d in enumerate(others)], local_sem=T.sem.sent)
+        count["sent"] = count.get("sent", 0) + len(others)
+
+    inc(sy.dma_start(T.cbt[:, 0:4 * G], T.cb[:]), "ldc", 16)
+    inc(ac.dma_start(T.xt[:, 0:768], T.x[:]), "ldx", 16)
+    inc(sy.dma_start(T.wt[:], T.w[:]), "ldw", 16)
+    inc(g.iota(T.pi[:], [[0, 1]], 0, 1), "io")
+    inc(g.iota(T.jj[:], [[1, 128]], 0, -1, allow_small_or_imprecise_dtypes=True), "io")
+    inc(ve.memset(T.cbt[:, 4 * G:512], 0.0), "dv")
+    inc(ve.memset(T.zt[:], 0.0), "z")
+    inc(ve.memset(T.xt[:, 768:896], 0.0), "dv")
+    inc(ve.memset(T.ab[:], 0.0), "dv")
+    wait(ac, "z")
+    for b in range(4):
+        inc(ac.activation(T.eb[:, 512 * b:512 * b + 512], T.zt[:], Act.Copy), "eb")
+    wait(ve, "dv", "ldc")
+    inc(quant("cw0", 0, 128, T.cbt[:]), "q0")
+    wait(g, "q0")
+    to_all((cc("cw0", 0, G), cc("call0", G * r, G * r + G)), "arrc0")
+    to_all((sc("cw0", 0, G), sc("call0", G * r, G * r + G)), "arrc0")
+    inc(g.iota(T.idb[:], [[TOK, N], [0, 2]], 0, 0, allow_small_or_imprecise_dtypes=True), "io")
+    wait(ve, "io")
+    inc(ve.tensor_scalar(T.pg[:], T.pi[:], G - 1, None, Op.bitwise_and), "dv")
+    wait(ve, "dv")
+    inc(ve.tensor_copy(T.gcol[:], T.pg[:]), "dv")
+    inc(ve.tensor_copy(T.own16[:, 0:1], T.pg[:]), "dv")
+    wait(ve, "ldx")
+    inc(quant("xq", 0, 224, T.xt[:]), "qx")
+    wait(ve, "dv", "q0")
+    wait(ac, "dv", "q0")
+    inc(pickc("call0", G * r, G * r + G, "cw0", 0, G, T.own16[:, 0:1]), "own")
+    inc(picks("call0", G * r, G * r + G, "cw0", 0, G, T.own16[:, 0:1]), "own")
+    inc(ve.memset(T.zf[:], 0.0), "dv")
+    inc(ve.memset(T.hb[:], 0.0), "dv")
+    inc(ve.memset(T.ub[:], 0.0), "dv")
+    inc(ve.memset(T.fb[:], 0.0), "dv")
+    inc(ve.memset(T.ob[:], 0.0), "dv")
+    inc(ve.memset(T.rst[:], 1.0), "dv")
+    for q in range(4):
+        for e in range(4):
+            a = 512 * q + 4 * (4 * q + e) + e
+            inc(ve.memset(T.ab[0:TOK, a:512 * q + 512:64], -1.0), "dv")
+    wait(ve, "dv", "eb")
+    inc(ve.memset(T.hb[:, 0:1], 1.0), "dv")
+    inc(ve.memset(T.hb[:, 512:513], 1.0), "dv")
+    inc(ve.memset(T.ob[0:TOK, 0:512:4], -1.0), "dv")
+    inc(ve.memset(T.rst[:, 0:48:16], 0.0), "dv")
+    inc(ve.tensor_scalar(T.ub[0:TOK, 0:512:4], T.jj[0:TOK, :], 0.0, None, Op.is_ge), "dv")
+    inc(ve.tensor_scalar(T.ub[0:TOK, 1:512:4], T.jj[0:TOK, :], 0.0, -1.0, Op.is_ge, Op.mult), "dv")
+    for b in range(4):
+        inc(ve.tensor_scalar(T.eb[:, 512 * b + b:512 * b + 512:4], T.jj[:], 0.0, 0.25, Op.is_equal, Op.mult), "dv")
+    wait(ve, "dv", "z")
+    inc(quant("uq", 0, 128, T.ub[:]), "qk")
+    inc(quant("oq", 0, 128, T.ob[:]), "qk")
+    inc(quant("aq", 0, 512, T.ab[:]), "qk")
+    inc(quant("eq", 0, 512, T.eb[:]), "qk")
+    inc(quant("fa", 64, 192, T.zt[:]), "qk")
+    inc(quant("fo", 64, 192, T.zt[:]), "qk")
+    late = [False]
+
+    def late_setup():
+        inc(ve.memset(T.nt[:], 0.0), "dv")
+        inc(quant("pick", 16, 144, T.zt[:]), "qk")
+        inc(quant("land0", LW, LW + 128, T.zt[:]), "qk")
+        inc(quant("land1", LW, LW + 128, T.zt[:]), "qk")
+        inc(quant("cw1", 0, 128, T.zt[:]), "qk")
+        wait(ve, "ldw", "qk")
+        inc(quant("wq", 0, 128, T.wt[:]), "qw")
+
+    def unpack(t):
+        for b in range(4):
+            call = mm(T.psn[:, 512 * b:512 * b + 128], "eq", 128 * b, "cw%d" % t, 0, 128)
+            inc(call, "dd")
+        wait(ac, "dd")
+        for b in range(4):
+            inc(ac.activation(T["dc%d" % t][:, b:4 * G:4], T.psn[:, 512 * b:512 * b + G], Act.Copy, scale=2.0), "dc")
+
+    wait(te, "q0", "qk")
+    unpack(0)
+
+    for t in range(R):
+        call_, cw, cn = "call%d" % t, "cw%d" % t, "cw%d" % (t + 1)
+        slot, land, v, lists = "slot%d" % t, "land%d" % t, T["v%d" % t], T["lists%d" % t]
+        x0 = TOK * t
+        if t == 0:
+            wait(te, "qx")
+        wait(te, "own")
+        te.wait_ge(T.sem["arrc%d" % t], sum(2 * len(topo.engines(T.cores[d], core)) for d in others))
+        inc(mm(T.pss[:, 0:128], "xq", x0, call_, 0, 128), "s")
+        wait(ve, "s")
+        inc(ve.tensor_tensor_scan(T.cm[:], T.pss[:, 0:128], T.zf[:], -1e29, Op.max, Op.add), "cm")
+        wait(ve, "cm", "dv")
+        wait(ac, "cm", "dv")
+        best = T.cm[:, 127:128]
+        inc(ve.tensor_scalar(T.hb[:, 4:512:4], T.cm[:, 0:127], best, None, Op.is_lt), "h")
+        inc(ac.activation(T.hb[:, 1:512:4], T.cm[:], Act.Sign, bias=best, scale=-1.0), "h")
+        inc(ve.tensor_scalar(T.hb[:, 516:544:4], T.cm[:, 15:127:16], best, None, Op.is_lt), "h")
+        inc(ac.activation(T.hb[:, 513:544:4], T.cm[:, 15:128:16], Act.Sign, bias=best, scale=-1.0), "h")
+        wait(ve, "h")
+        inc(quant("hq", 0, 136, T.hb[:]), "hq")
+        wait(te, "hq")
+        if t:
+            wait(te, "yc")
+        inc(mm(T.psp[:, 0:136], "uq", 0, "hq", 0, 136), "pc")
+        wait(ve, "pc")
+        inc(ve.tensor_scalar(T.fb[:, 0:128], T.psp[:, 0:128], 1.0, None, Op.is_ge), "dv")
+        inc(ve.tensor_scalar(T.fb[:, 128:256], T.psp[:, 0:128], 2.0, None, Op.is_ge), "dv")
+        inc(ve.tensor_scalar(T.fb[:, 256:288:4], T.psp[:, 128:136], float(CAPP + 1), None, Op.is_ge), "dv")
+        wait(ve, "dv")
+        inc(quant("fa", 0, 128, T.fb[:, 0:512]), "fa")
+        inc(quant("fo", 0, 128, T.fb[:, 4:516]), "fo")
+        wait(te, "fa")
+        inc(mm(T.psl[:, 0:128], "oq", 0, "fa", 64, 192), "lim")
+        mm(T.psf[:, 0:128], "aq", 0, "fa", 0, 128, True, False)
+        mm(T.psf[:, 0:128], "aq", 256, "fa", 2, 130, False, False)
+        wait(te, "fo")
+        mm(T.psf[:, 0:128], "aq", 128, "fo", 0, 128, False, False)
+        inc(mm(T.psf[:, 0:128], "aq", 384, "fo", 2, 130, False, True), "fs")
+        wait(ve, "lim")
+        inc(ve.tensor_copy(T.lm[:], T.psl[:, 0:8]), "dv")
+        wait(ve, "dv", "fs")
+        for i in range(2):
+            inc(ve.tensor_tensor(T.vd[:, i:16:2], T.psf[:, 32 * i:32 * i + 32:4], T.lm[:], Op.is_lt), "dv")
+        wait(ve, "dv")
+        for i in range(2):
+            inc(ve.tensor_tensor(T.vz[:, i:16:2], T.psf[:, 32 * i:32 * i + 32:4], T.vd[:, i:16:2], Op.mult), "dv")
+        wait(ve, "dv")
+        inc(ve.tensor_scalar(v[:], T.vz[:], float(TOK), None, Op.add), "v")
+        wait(ve, "v")
+        wait(ac, "v")
+        wait(g, "v")
+        to_each(lambda d: v[:, 2 * d:2 * d + 2], lists[:, 2 * r:2 * r + 2], "arrl%d" % t)
+        inc(pickc(slot, 0, LW, "xq", x0, 224, v[:]), "pk")
+        inc(picks(slot, 0, LW, "xq", x0, 224, v[:]), "pks")
+        wait(g, "pk")
+        to_each(lambda d: cc(slot, C2 * d, C2 * d + C2), cc(land, C2 * r, C2 * r + C2), "arrt%d" % t)
+        wait(g, "pks")
+        to_each(lambda d: sc(slot, C2 * d, C2 * d + C2), sc(land, C2 * r, C2 * r + C2), "arrt%d" % t)
+        inc(pickc(land, C2 * r, C2 * r + C2, "xq", x0, 224, v[:, 2 * r:2 * r + 2]), "ol")
+        inc(picks(land, C2 * r, C2 * r + C2, "xq", x0, 224, v[:, 2 * r:2 * r + 2]), "ol")
+        if t == 0:
+            late_setup()
+        def take(src, a, b):
+            if a < b:
+                inc(ve.tensor_scalar(T.rv[:, a:b], src[:, a:b], TOK - 0.5, None, Op.is_lt), "dv")
+                inc(ve.tensor_scalar(T.lf[:, a:b], src[:, a:b], 1.0, None, Op.add), "dv")
+        take(v, 2 * r, 2 * r + 2)
+        ve.wait_ge(T.sem["arrl%d" % t], len(others))
+        take(lists, 0, 2 * r)
+        take(lists, 2 * r + 2, 16)
+        wait(ve, "dv")
+        inc(ve.tensor_tensor_scan(T.cum[:], T.rv[:], T.zf[:, 0:16], 0.0, Op.add, Op.add), "dv")
+        inc(ve.tensor_tensor(T.num[:], T.lf[:], T.idb[:], Op.add), "dv")
+        wait(ve, "dv")
+        inc(ve.tensor_scalar(T.thr[:], T.cum[:, 15:16], 2.0, None, Op.min), "dv")
+        inc(ve.tensor_scalar(T.mv[:], T.cum[:, 15:16], 1.0, float(G), Op.min, Op.mult), "dv")
+        inc(ve.tensor_scalar(T.lt[:, 0:16], T.cum[:], 1.0, None, Op.is_lt), "dv")
+        inc(ve.tensor_scalar(T.lt[:, 32:48], T.cum[:], 2.0, None, Op.is_lt), "dv")
+        wait(ve, "dv")
+        inc(ve.tensor_scalar(T.lt[:, 16:32], T.cum[:], T.thr[:], None, Op.is_lt), "dv")
+        inc(ve.tensor_scalar(T.fin[:, 0:1], T.mv[:], T.gcol[:], None, Op.add), "dv")
+        wait(ve, "dv")
+        inc(ve.tensor_tensor_scan(T.sc[:], T.rst[:], T.lt[:], 0.0, Op.mult, Op.add), "dv")
+        inc(ve.tensor_tensor(T.numv[:], T.num[:], T.rv[:], Op.mult), "dv")
+        wait(ve, "dv")
+        inc(ve.tensor_scalar(T.po[:, 0:3], T.sc[:, 15:48:16], float(G), T.gcol[:], Op.mult, Op.add), "dv")
+        inc(ve.tensor_scalar(T.eq1[:], T.cum[:], 1.0, None, Op.is_equal), "dv")
+        inc(ve.tensor_scalar(T.eq2[:], T.cum[:], 2.0, None, Op.is_equal), "dv")
+        for q in (ve, ac):
+            wait(q, "dv", "ol", "qk")
+            q.wait_ge(T.sem["arrt%d" % t], 2 * len(others))
+        inc(pickc("pick", 0, 48, land, 0, LW + G, T.po[:, 0:3]), "pp")
+        inc(picks("pick", 0, 48, land, 0, LW + G, T.po[:, 0:3]), "pp")
+        wait(te, "pp", "dc", "qw")
+        for b in range(4):
+            bank = T.psn[:, 512 * b:512 * b + 128]
+            mm(bank, "eq", 128 * b, "pick", 0, 128, True, False)
+            inc(mm(bank, "eq", 128 * b, "pick", 16, 144, False, True), "n%d" % b)
+        inc(mm(T.psp[:, 0:128], "wq", 0, "pick", 0, 128), "y")
+        inc(ve.tensor_tensor(T.id1[:], T.numv[:], T.eq1[:], Op.mult), "dv")
+        inc(ve.tensor_tensor(T.id2[:], T.numv[:], T.eq2[:], Op.mult), "dv")
+        wait(ve, "dv")
+        inc(ve.tensor_reduce(T.idr[:, 0:1], T.id1[:], AxisListType.X, Op.add), "dv")
+        inc(ve.tensor_reduce(T.idr[:, 1:2], T.id2[:], AxisListType.X, Op.add), "dv")
+        wait(ve, "dv", "dc")
+        inc(ve.tensor_scalar(T["idt%d" % t][:], T.idr[:], -1.0, None, Op.add), "id")
+        for b in range(4):
+            wait(ve, "n%d" % b)
+            inc(ve.tensor_tensor(T.nt[:, b:4 * G:4], T.psn[:, 512 * b:512 * b + G], T["dc%d" % t][:, b:4 * G:4], Op.add), "dv")
+        wait(ve, "dv")
+        inc(quant(cw, G, G + 128, T.nt[:]), "wn")
+        wait(ac, "y")
+        for i in range(2):
+            inc(ac.activation(T.ysb[:, 32 * t + i:32 * t + 32:2], T.psp[:, 32 * i:32 * i + G], Act.Copy), "yc")
+        for q in (ve, ac):
+            wait(q, "wn")
+        inc(pickc(cn, 0, G, cw, 0, C2, T.fin[:, 0:1]), "cn")
+        inc(picks(cn, 0, G, cw, 0, C2, T.fin[:, 0:1]), "cns")
+        wait(sy, "id")
+        inc(sy.dma_start(T.ids[0:1, 32 * t:32 * t + 32], T["idt%d" % t][0:G, 0:2]), "out", 16)
+        wait(sy, "yc")
+        inc(sy.dma_start(T.y[:, 32 * t:32 * t + 32], T.ysb[:, 32 * t:32 * t + 32]), "out", 16)
+        if t + 1 < R:
+            nxt = "call%d" % (t + 1)
+            wait(g, "cn")
+            to_all((cc(cn, 0, G), cc(nxt, G * r, G * r + G)), "arrc%d" % (t + 1))
+            wait(g, "cns")
+            to_all((sc(cn, 0, G), sc(nxt, G * r, G * r + G)), "arrc%d" % (t + 1))
+            inc(pickc(nxt, G * r, G * r + G, cw, 0, C2, T.fin[:, 0:1]), "own")
+            inc(picks(nxt, G * r, G * r + G, cw, 0, C2, T.fin[:, 0:1]), "own")
+            wait(te, "cn", "cns")
+            unpack(t + 1)
+    wait(sy, "cn", "cns")
+    inc(sy.dma_start(T.oc[:], cc("cw%d" % R, 0, G)), "out", 16)
+    wait(ac, "cns")
+    for k in range(4):
+        q, s = ((sy, "out"), (ac, "outs"))[k % 2 if k else 1]
+        inc(q.dma_start(T.osc[4 * k:4 * k + 4, :], T["cw%ds" % R][32 * k:32 * k + 4, 0:G]), s, 16)
+    for name in count:
+        if seen.get(name, 0) < count[name]:
+            wait(g, name)

@@ -2,11 +2,10 @@ from concourse.bass import DstId, RemoteDMATransfer
 from concourse.mybir import dt, AluOpType as Op, AxisListType, ActivationFunctionType as Act
 
 N, G, TOK, CAPP, R = 8, 16, 96, 32, 2
-K = N * G
 C2 = 2 * G
 LW = N * C2
 
-_F, _B, _U, _Q, _S = "float32", "bfloat16", "uint16", "float8_e4m3fn_x4", "uint8"
+_F, _B, _U, _I, _Q, _S = "float32", "bfloat16", "uint16", "int32", "float8_e4m3fn_x4", "uint8"
 SCRATCH = {}
 
 
@@ -19,28 +18,29 @@ def _mx(name, n):
     _buf(name + "s", n, _S)
 
 
-for _n, _w in (("cbt", 512), ("xt", 896), ("wt", 512), ("zt", 512), ("ub", 512), ("ab", 2048), ("ob", 512),
+for _n, _w in (("cbt", 512), ("xt", 896), ("wt", 512), ("zt", 512), ("ub", 512), ("ab", 2048), ("ob", 512), ("m16", 512),
                ("eb", 2048), ("hb", 544), ("fb", 516), ("nt", 512)):
     _buf(_n, _w, _B)
 for _n, _w in (("xq", 224), ("wq", 128), ("uq", 128), ("aq", 512), ("oq", 128), ("eq", 512), ("hq", 136), ("fa", 192),
                ("fo", 192), ("cw0", 144), ("cw1", 144), ("cw2", 16), ("call0", 128), ("call1", 128), ("slot0", 256),
                ("slot1", 256), ("land0", 384), ("land1", 384), ("pick", 144)):
     _mx(_n, _w)
-for _n, _w in (("jj", 128), ("zf", 128), ("cm", 128), ("lm", 8), ("vd", 16), ("vz", 16), ("gcol", 1), ("rst", 48), ("rv", 16),
-               ("cum", 16), ("lt", 48), ("sc", 48), ("thr", 1), ("mv", 1), ("lf", 16), ("idb", 16), ("num", 16), ("numv", 16),
+for _n, _w in (("jj", 128), ("zf", 128), ("cm", 128), ("gcol", 1), ("rst", 48), ("rv", 16),
+               ("cum", 16), ("lt", 48), ("sc", 48), ("thr", 1), ("mv", 1), ("num", 16), ("numv", 16),
                ("eq1", 16), ("eq2", 16), ("id1", 16), ("id2", 16), ("idr", 2), ("idt0", 2), ("idt1", 2), ("dc0", 64), ("dc1", 64),
                ("ysb", 64)):
     _buf(_n, _w, _F)
-for _n, _w in (("v0", 16), ("v1", 16), ("lists0", 16), ("lists1", 16), ("po", 4), ("fin", 2), ("own16", 2)):
+for _n, _w in (("v0", 16), ("v1", 16), ("lst0", 16), ("lst1", 16), ("lists0", 16), ("lists1", 16), ("po", 4), ("fin", 2),
+               ("own16", 2)):
     _buf(_n, _w, _U)
-_buf("pi", 1, "int32")
-_buf("pg", 1, "int32")
-for _n, _w in (("pss", 512), ("psp", 512), ("psl", 512), ("psf", 512), ("psn", 2048)):
+for _n, _w in (("pi", 1), ("pg", 1), ("xi", 16), ("xa", 16), ("li", 16), ("lf", 16), ("ll", 16), ("idb", 16)):
+    _buf(_n, _w, _I)
+for _n, _w in (("pss", 512), ("psp", 512), ("psf", 512), ("psn", 2048)):
     SCRATCH[_n] = ("psum", [128, _w], _F)
 
-SEMAPHORES = ["ldc", "ldx", "ldw", "io", "dv", "z", "eb", "q0", "qx", "qw", "qk", "own", "arrc0", "arrc1", "arrl0", "arrl1",
-              "arrt0", "arrt1", "sent", "s", "cm", "h", "hq", "pc", "fa", "fo", "lim", "fs", "v", "pk", "pks", "ol", "pp",
-              "n0", "n1", "n2", "n3", "y", "yc", "wn", "cn", "cns", "dd", "dc", "id", "out", "outs"]
+SEMAPHORES = ["ldc", "ldx", "ldw", "io", "io2", "dv", "z", "zc", "za", "zu", "ze", "kb", "ku", "ka", "ke", "q0", "qx", "qw", "own",
+              "arrc0", "arrc1", "arrl0", "arrl1", "arrt0", "arrt1", "sent", "s", "cm", "h", "hq", "pc", "fa", "fo", "fs",
+              "l", "v", "pk", "pks", "ol", "pp", "n0", "n1", "n2", "n3", "y", "yc", "wn", "cn", "cns", "dd", "dc", "id", "out", "outs"]
 
 
 def rank_program(g, core, T, topo):
@@ -83,169 +83,203 @@ def rank_program(g, core, T, topo):
     for d in others:
         rid, pid = topo.addr(T.cores[d], core)
         dest[d] = DstId(rid=rid, pnc=pid)
-    engs = {d: topo.engines(core, T.cores[d]) for d in others}
+
+    def rest_of(s):
+        return [d for d in range(N) if d != s]
+
+    def engines(s):
+        return topo.engines(T.cores[s], T.cores[rest_of(s)[0]])
+
+    def deal(s, kind):
+        o, e = rest_of(s), engines(s)
+        w, h = len(e) // 4, len(e) // 2
+        f = e[h:] + e[:h] if kind else e
+        return [{o[i]: e[w * i:w * i + w] for i in range(4)}, {o[4]: f[0:w], o[5]: f[w:h], o[6]: f[h:]}]
+
+    def fused(parts, src, dst, sem):
+        g.remote_dma_fused([RemoteDMATransfer(dst_ids=[dest[d]], dma_engine_mask=sum(1 << e for e in es), remote_sem=T.sem[sem],
+                                              srcs=[src(d)], dsts=[dst]) for d, es in parts.items()], local_sem=T.sem.sent)
+        count["sent"] = count.get("sent", 0) + sum(len(es) for es in parts.values())
 
     def to_all(view, sem):
-        g.remote_dma_fused([RemoteDMATransfer(dst_ids=[dest[d] for d in others], dma_engine_mask=topo.mask(core, T.cores[others[0]]),
+        es = engines(r)
+        g.remote_dma_fused([RemoteDMATransfer(dst_ids=[dest[d] for d in others], dma_engine_mask=sum(1 << e for e in es),
                                               remote_sem=T.sem[sem], srcs=[view[0]], dsts=[view[1]] * len(others))],
                            local_sem=T.sem.sent)
-        count["sent"] = count.get("sent", 0) + len(engs[others[0]])
+        count["sent"] = count.get("sent", 0) + len(es)
 
-    def to_each(src, dst, sem):
-        g.remote_dma_fused([RemoteDMATransfer(dst_ids=[dest[d]], dma_engine_mask=1 << engs[d][i], remote_sem=T.sem[sem],
-                                              srcs=[src(d)], dsts=[dst]) for i, d in enumerate(others)], local_sem=T.sem.sent)
-        count["sent"] = count.get("sent", 0) + len(others)
+    arrive_c = sum(2 * len(engines(s)) for s in others)
+    arrive_t = sum(len(p[r]) for s in others for kind in range(2) for p in deal(s, kind) if r in p)
 
     inc(sy.dma_start(T.cbt[:, 0:4 * G], T.cb[:]), "ldc", 16)
     inc(ac.dma_start(T.xt[:, 0:768], T.x[:]), "ldx", 16)
     inc(sy.dma_start(T.wt[:], T.w[:]), "ldw", 16)
     inc(g.iota(T.pi[:], [[0, 1]], 0, 1), "io")
     inc(g.iota(T.jj[:], [[1, 128]], 0, -1, allow_small_or_imprecise_dtypes=True), "io")
-    inc(ve.memset(T.cbt[:, 4 * G:512], 0.0), "dv")
+    inc(g.iota(T.m16[:], [[0, 8], [1, 16], [-1, 4]], 0, 0, allow_small_or_imprecise_dtypes=True), "io")
     inc(ve.memset(T.zt[:], 0.0), "z")
-    inc(ve.memset(T.xt[:, 768:896], 0.0), "dv")
-    inc(ve.memset(T.ab[:], 0.0), "dv")
+    inc(ve.memset(T.cbt[:, 4 * G:512], 0.0), "zc")
+    inc(ve.memset(T.xt[:, 768:896], 0.0), "za")
+    inc(ve.memset(T.hb[:], 0.0), "za")
+    inc(ve.memset(T.fb[:], 0.0), "za")
+    inc(ve.memset(T.zf[:], 0.0), "za")
+    wait(ve, "z")
+    inc(quant("fa", 64, 192, T.zt[:]), "ka")
+    inc(quant("fo", 64, 192, T.zt[:]), "ka")
     wait(ac, "z")
-    for b in range(4):
-        inc(ac.activation(T.eb[:, 512 * b:512 * b + 512], T.zt[:], Act.Copy), "eb")
-    wait(ve, "dv", "ldc")
+    inc(ac.activation(T.ub[:], T.zt[:], Act.Copy), "zu")
+    inc(ac.activation(T.ob[:], T.zt[:], Act.Copy), "zu")
+    wait(ve, "zc", "ldc")
     inc(quant("cw0", 0, 128, T.cbt[:]), "q0")
     wait(g, "q0")
     to_all((cc("cw0", 0, G), cc("call0", G * r, G * r + G)), "arrc0")
     to_all((sc("cw0", 0, G), sc("call0", G * r, G * r + G)), "arrc0")
-    inc(g.iota(T.idb[:], [[TOK, N], [0, 2]], 0, 0, allow_small_or_imprecise_dtypes=True), "io")
+    inc(g.iota(T.idb[:], [[TOK, N], [0, 2]], 1, 0), "io2")
+    wait(ve, "za", "ldx")
+    inc(quant("xq", 0, 224, T.xt[:]), "qx")
     wait(ve, "io")
     inc(ve.tensor_scalar(T.pg[:], T.pi[:], G - 1, None, Op.bitwise_and), "dv")
-    wait(ve, "dv")
+    inc(ve.memset(T.hb[0:TOK, 0:1], 1.0), "za")
+    inc(ve.memset(T.hb[0:TOK, 512:513], 1.0), "za")
+    wait(ve, "dv", "zu")
     inc(ve.tensor_copy(T.gcol[:], T.pg[:]), "dv")
     inc(ve.tensor_copy(T.own16[:, 0:1], T.pg[:]), "dv")
-    wait(ve, "ldx")
-    inc(quant("xq", 0, 224, T.xt[:]), "qx")
+    inc(ve.tensor_scalar(T.ub[:, 0:512:4], T.jj[:], 0.0, None, Op.is_ge), "kb")
+    inc(ve.tensor_scalar(T.ub[:, 1:512:4], T.jj[:], 0.0, -1.0, Op.is_ge, Op.mult), "kb")
+    inc(ve.memset(T.ob[:, 0:512:4], 128.0), "kb")
     wait(ve, "dv", "q0")
     wait(ac, "dv", "q0")
     inc(pickc("call0", G * r, G * r + G, "cw0", 0, G, T.own16[:, 0:1]), "own")
     inc(picks("call0", G * r, G * r + G, "cw0", 0, G, T.own16[:, 0:1]), "own")
-    inc(ve.memset(T.zf[:], 0.0), "dv")
-    inc(ve.memset(T.hb[:], 0.0), "dv")
-    inc(ve.memset(T.ub[:], 0.0), "dv")
-    inc(ve.memset(T.fb[:], 0.0), "dv")
-    inc(ve.memset(T.ob[:], 0.0), "dv")
-    inc(ve.memset(T.rst[:], 1.0), "dv")
-    for q in range(4):
-        for e in range(4):
-            a = 512 * q + 4 * (4 * q + e) + e
-            inc(ve.memset(T.ab[0:TOK, a:512 * q + 512:64], -1.0), "dv")
-    wait(ve, "dv", "eb")
-    inc(ve.memset(T.hb[:, 0:1], 1.0), "dv")
-    inc(ve.memset(T.hb[:, 512:513], 1.0), "dv")
-    inc(ve.memset(T.ob[0:TOK, 0:512:4], -1.0), "dv")
-    inc(ve.memset(T.rst[:, 0:48:16], 0.0), "dv")
-    inc(ve.tensor_scalar(T.ub[0:TOK, 0:512:4], T.jj[0:TOK, :], 0.0, None, Op.is_ge), "dv")
-    inc(ve.tensor_scalar(T.ub[0:TOK, 1:512:4], T.jj[0:TOK, :], 0.0, -1.0, Op.is_ge, Op.mult), "dv")
     for b in range(4):
-        inc(ve.tensor_scalar(T.eb[:, 512 * b + b:512 * b + 512:4], T.jj[:], 0.0, 0.25, Op.is_equal, Op.mult), "dv")
-    wait(ve, "dv", "z")
-    inc(quant("uq", 0, 128, T.ub[:]), "qk")
-    inc(quant("oq", 0, 128, T.ob[:]), "qk")
-    inc(quant("aq", 0, 512, T.ab[:]), "qk")
-    inc(quant("eq", 0, 512, T.eb[:]), "qk")
-    inc(quant("fa", 64, 192, T.zt[:]), "qk")
-    inc(quant("fo", 64, 192, T.zt[:]), "qk")
-    late = [False]
-
-    def late_setup():
-        inc(ve.memset(T.nt[:], 0.0), "dv")
-        inc(quant("pick", 16, 144, T.zt[:]), "qk")
-        inc(quant("land0", LW, LW + 128, T.zt[:]), "qk")
-        inc(quant("land1", LW, LW + 128, T.zt[:]), "qk")
-        inc(quant("cw1", 0, 128, T.zt[:]), "qk")
-        wait(ve, "ldw", "qk")
-        inc(quant("wq", 0, 128, T.wt[:]), "qw")
+        inc(ac.activation(T.eb[:, 512 * b:512 * b + 512], T.zt[:], Act.Copy), "ze")
+    inc(ac.activation(T.nt[:], T.zt[:], Act.Copy), "ze")
+    wait(ve, "kb")
+    inc(quant("uq", 0, 128, T.ub[:]), "ku")
+    for q in range(4):
+        inc(ve.tensor_scalar(T.ab[:, 512 * q:512 * q + 512], T.m16[:], 4.0 * q, None, Op.is_equal), "kb")
+    inc(quant("oq", 0, 128, T.ob[:]), "ka")
+    wait(ve, "kb")
+    inc(quant("aq", 0, 512, T.ab[:]), "ka")
 
     def unpack(t):
         for b in range(4):
-            call = mm(T.psn[:, 512 * b:512 * b + 128], "eq", 128 * b, "cw%d" % t, 0, 128)
-            inc(call, "dd")
+            inc(mm(T.psn[:, 512 * b:512 * b + 128], "eq", 128 * b, "cw%d" % t, 0, 128), "dd")
         wait(ac, "dd")
         for b in range(4):
             inc(ac.activation(T["dc%d" % t][:, b:4 * G:4], T.psn[:, 512 * b:512 * b + G], Act.Copy, scale=2.0), "dc")
 
-    wait(te, "q0", "qk")
-    unpack(0)
+    def late_setup():
+        wait(ve, "ze")
+        for b in range(4):
+            inc(ve.tensor_scalar(T.eb[:, 512 * b + b:512 * b + 512:4], T.jj[:], 0.0, 0.25, Op.is_equal, Op.mult), "dv")
+        inc(ve.memset(T.rst[:], 1.0), "dv")
+        wait(ve, "dv")
+        inc(ve.memset(T.rst[:, 0:48:16], 0.0), "dv")
+        inc(quant("eq", 0, 512, T.eb[:]), "ke")
+        inc(quant("pick", 16, 144, T.zt[:]), "ke")
+        inc(quant("land0", LW, LW + 128, T.zt[:]), "ke")
+        wait(te, "q0", "ke")
+        unpack(0)
+
+    def rest_setup():
+        inc(quant("cw1", G, G + 128, T.zt[:]), "ke")
+        wait(ve, "ldw")
+        inc(quant("wq", 0, 128, T.wt[:]), "qw")
+        inc(quant("land1", LW, LW + 128, T.zt[:]), "ke")
+
+    def results(t):
+        wait(te, "qw")
+        inc(mm(T.psp[:, 0:128], "wq", 0, "pick", 0, 128), "y")
+        wait(ac, "y")
+        for i in range(2):
+            inc(ac.activation(T.ysb[:, C2 * t + i:C2 * t + C2:2], T.psp[:, 32 * i:32 * i + G], Act.Copy), "yc")
+        wait(sy, "yc")
+        inc(sy.dma_start(T.y[:, C2 * t:C2 * t + C2], T.ysb[:, C2 * t:C2 * t + C2]), "out", 16)
 
     for t in range(R):
         call_, cw, cn = "call%d" % t, "cw%d" % t, "cw%d" % (t + 1)
-        slot, land, v, lists = "slot%d" % t, "land%d" % t, T["v%d" % t], T["lists%d" % t]
+        slot, land, v, lst, lists = "slot%d" % t, "land%d" % t, T["v%d" % t], T["lst%d" % t], T["lists%d" % t]
         x0 = TOK * t
         if t == 0:
-            wait(te, "qx")
+            wait(te, "qx", "ku")
         wait(te, "own")
-        te.wait_ge(T.sem["arrc%d" % t], sum(2 * len(topo.engines(T.cores[d], core)) for d in others))
+        te.wait_ge(T.sem["arrc%d" % t], arrive_c)
         inc(mm(T.pss[:, 0:128], "xq", x0, call_, 0, 128), "s")
-        wait(ve, "s")
+        wait(ve, "za", "s")
         inc(ve.tensor_tensor_scan(T.cm[:], T.pss[:, 0:128], T.zf[:], -1e29, Op.max, Op.add), "cm")
-        wait(ve, "cm", "dv")
-        wait(ac, "cm", "dv")
-        best = T.cm[:, 127:128]
-        inc(ve.tensor_scalar(T.hb[:, 4:512:4], T.cm[:, 0:127], best, None, Op.is_lt), "h")
-        inc(ac.activation(T.hb[:, 1:512:4], T.cm[:], Act.Sign, bias=best, scale=-1.0), "h")
-        inc(ve.tensor_scalar(T.hb[:, 516:544:4], T.cm[:, 15:127:16], best, None, Op.is_lt), "h")
-        inc(ac.activation(T.hb[:, 513:544:4], T.cm[:, 15:128:16], Act.Sign, bias=best, scale=-1.0), "h")
+        wait(ve, "cm")
+        wait(ac, "za", "cm")
+        best = T.cm[0:TOK, 127:128]
+        inc(ve.tensor_scalar(T.hb[0:TOK, 4:512:4], T.cm[0:TOK, 0:127], best, None, Op.is_lt), "h")
+        inc(ac.activation(T.hb[0:TOK, 1:512:4], T.cm[0:TOK, :], Act.Sign, bias=best, scale=-1.0), "h")
+        inc(ve.tensor_scalar(T.hb[0:TOK, 516:544:4], T.cm[0:TOK, 15:127:16], best, None, Op.is_lt), "h")
+        inc(ac.activation(T.hb[0:TOK, 513:544:4], T.cm[0:TOK, 15:128:16], Act.Sign, bias=best, scale=-1.0), "h")
         wait(ve, "h")
         inc(quant("hq", 0, 136, T.hb[:]), "hq")
-        wait(te, "hq")
         if t:
             wait(te, "yc")
+        wait(te, "hq")
         inc(mm(T.psp[:, 0:136], "uq", 0, "hq", 0, 136), "pc")
+        if t == 0:
+            wait(te, "ka")
         wait(ve, "pc")
-        inc(ve.tensor_scalar(T.fb[:, 0:128], T.psp[:, 0:128], 1.0, None, Op.is_ge), "dv")
-        inc(ve.tensor_scalar(T.fb[:, 128:256], T.psp[:, 0:128], 2.0, None, Op.is_ge), "dv")
-        inc(ve.tensor_scalar(T.fb[:, 256:288:4], T.psp[:, 128:136], float(CAPP + 1), None, Op.is_ge), "dv")
+        inc(ve.tensor_scalar(T.fb[0:TOK, 0:128], T.psp[0:TOK, 0:128], 1.0, None, Op.is_lt), "dv")
+        inc(ve.tensor_scalar(T.fb[0:TOK, 128:256], T.psp[0:TOK, 0:128], 2.0, None, Op.is_lt), "dv")
+        for i in range(2):
+            inc(ve.tensor_scalar(T.fb[0:TOK, 256 + 128 * i:384 + 128 * i:16], T.psp[0:TOK, 128:136], float(CAPP + 1), None, Op.is_lt), "dv")
         wait(ve, "dv")
         inc(quant("fa", 0, 128, T.fb[:, 0:512]), "fa")
         inc(quant("fo", 0, 128, T.fb[:, 4:516]), "fo")
         wait(te, "fa")
-        inc(mm(T.psl[:, 0:128], "oq", 0, "fa", 64, 192), "lim")
-        mm(T.psf[:, 0:128], "aq", 0, "fa", 0, 128, True, False)
-        mm(T.psf[:, 0:128], "aq", 256, "fa", 2, 130, False, False)
+        ps = T.psf[:, 0:128]
+        mm(ps, "aq", 0, "fa", 0, 128, True, False)
+        mm(ps, "aq", 256, "fa", 2, 130, False, False)
+        mm(ps, "oq", 0, "fa", 64, 192, False, False)
         wait(te, "fo")
-        mm(T.psf[:, 0:128], "aq", 128, "fo", 0, 128, False, False)
-        inc(mm(T.psf[:, 0:128], "aq", 384, "fo", 2, 130, False, True), "fs")
-        wait(ve, "lim")
-        inc(ve.tensor_copy(T.lm[:], T.psl[:, 0:8]), "dv")
-        wait(ve, "dv", "fs")
+        mm(ps, "aq", 128, "fo", 0, 128, False, False)
+        inc(mm(ps, "aq", 384, "fo", 2, 130, False, True), "fs")
+        wait(ve, "fs")
         for i in range(2):
-            inc(ve.tensor_tensor(T.vd[:, i:16:2], T.psf[:, 32 * i:32 * i + 32:4], T.lm[:], Op.is_lt), "dv")
+            inc(ve.tensor_copy(lst[:, i:16:2], T.psf[:, 32 * i:32 * i + 32:4]), "l")
+        inc(ve.tensor_copy(T.xi[:], T.psf[:, 0:64:4]), "dv")
+        wait(g, "l")
+        fused({d: [engines(r)[i]] for i, d in enumerate(others)}, lambda d: lst[:, 2 * d:2 * d + 2], lists[:, 2 * r:2 * r + 2], "arrl%d" % t)
+        wait(ve, "dv")
+        inc(ve.tensor_scalar(T.xa[:], T.xi[:], 127, None, Op.bitwise_and), "dv")
         wait(ve, "dv")
         for i in range(2):
-            inc(ve.tensor_tensor(T.vz[:, i:16:2], T.psf[:, 32 * i:32 * i + 32:4], T.vd[:, i:16:2], Op.mult), "dv")
-        wait(ve, "dv")
-        inc(ve.tensor_scalar(v[:], T.vz[:], float(TOK), None, Op.add), "v")
+            inc(ve.tensor_copy(v[:, i:16:2], T.xa[:, 8 * i:8 * i + 8]), "v")
         wait(ve, "v")
         wait(ac, "v")
-        wait(g, "v")
-        to_each(lambda d: v[:, 2 * d:2 * d + 2], lists[:, 2 * r:2 * r + 2], "arrl%d" % t)
         inc(pickc(slot, 0, LW, "xq", x0, 224, v[:]), "pk")
         inc(picks(slot, 0, LW, "xq", x0, 224, v[:]), "pks")
         wait(g, "pk")
-        to_each(lambda d: cc(slot, C2 * d, C2 * d + C2), cc(land, C2 * r, C2 * r + C2), "arrt%d" % t)
+        for part in deal(r, 0):
+            fused(part, lambda d: cc(slot, C2 * d, C2 * d + C2), cc(land, C2 * r, C2 * r + C2), "arrt%d" % t)
         wait(g, "pks")
-        to_each(lambda d: sc(slot, C2 * d, C2 * d + C2), sc(land, C2 * r, C2 * r + C2), "arrt%d" % t)
+        for part in deal(r, 1):
+            fused(part, lambda d: sc(slot, C2 * d, C2 * d + C2), sc(land, C2 * r, C2 * r + C2), "arrt%d" % t)
         inc(pickc(land, C2 * r, C2 * r + C2, "xq", x0, 224, v[:, 2 * r:2 * r + 2]), "ol")
         inc(picks(land, C2 * r, C2 * r + C2, "xq", x0, 224, v[:, 2 * r:2 * r + 2]), "ol")
         if t == 0:
             late_setup()
         def take(src, a, b):
             if a < b:
-                inc(ve.tensor_scalar(T.rv[:, a:b], src[:, a:b], TOK - 0.5, None, Op.is_lt), "dv")
-                inc(ve.tensor_scalar(T.lf[:, a:b], src[:, a:b], 1.0, None, Op.add), "dv")
-        take(v, 2 * r, 2 * r + 2)
+                inc(ve.tensor_copy(T.li[:, a:b], src[:, a:b]), "dv")
+        wait(ve, "l")
+        take(lst, 2 * r, 2 * r + 2)
         ve.wait_ge(T.sem["arrl%d" % t], len(others))
         take(lists, 0, 2 * r)
         take(lists, 2 * r + 2, 16)
+        wait(ve, "dv", "io2")
+        inc(ve.tensor_scalar(T.lf[:], T.li[:], 127, None, Op.bitwise_and), "dv")
+        inc(ve.tensor_scalar(T.ll[:], T.li[:], 7, None, Op.logical_shift_right), "dv")
+        wait(ve, "dv")
+        inc(ve.tensor_tensor(T.rv[:], T.lf[:], T.ll[:], Op.is_lt), "dv")
+        inc(ve.tensor_tensor(T.num[:], T.lf[:], T.idb[:], Op.add), "dv")
         wait(ve, "dv")
         inc(ve.tensor_tensor_scan(T.cum[:], T.rv[:], T.zf[:, 0:16], 0.0, Op.add, Op.add), "dv")
-        inc(ve.tensor_tensor(T.num[:], T.lf[:], T.idb[:], Op.add), "dv")
         wait(ve, "dv")
         inc(ve.tensor_scalar(T.thr[:], T.cum[:, 15:16], 2.0, None, Op.min), "dv")
         inc(ve.tensor_scalar(T.mv[:], T.cum[:, 15:16], 1.0, float(G), Op.min, Op.mult), "dv")
@@ -262,16 +296,16 @@ def rank_program(g, core, T, topo):
         inc(ve.tensor_scalar(T.eq1[:], T.cum[:], 1.0, None, Op.is_equal), "dv")
         inc(ve.tensor_scalar(T.eq2[:], T.cum[:], 2.0, None, Op.is_equal), "dv")
         for q in (ve, ac):
-            wait(q, "dv", "ol", "qk")
-            q.wait_ge(T.sem["arrt%d" % t], 2 * len(others))
+            wait(q, "dv", "ol", "ke")
+            q.wait_ge(T.sem["arrt%d" % t], arrive_t)
+        wait(te, "dc")
         inc(pickc("pick", 0, 48, land, 0, LW + G, T.po[:, 0:3]), "pp")
         inc(picks("pick", 0, 48, land, 0, LW + G, T.po[:, 0:3]), "pp")
-        wait(te, "pp", "dc", "qw")
+        wait(te, "pp")
         for b in range(4):
             bank = T.psn[:, 512 * b:512 * b + 128]
             mm(bank, "eq", 128 * b, "pick", 0, 128, True, False)
             inc(mm(bank, "eq", 128 * b, "pick", 16, 144, False, True), "n%d" % b)
-        inc(mm(T.psp[:, 0:128], "wq", 0, "pick", 0, 128), "y")
         inc(ve.tensor_tensor(T.id1[:], T.numv[:], T.eq1[:], Op.mult), "dv")
         inc(ve.tensor_tensor(T.id2[:], T.numv[:], T.eq2[:], Op.mult), "dv")
         wait(ve, "dv")
@@ -284,17 +318,14 @@ def rank_program(g, core, T, topo):
             inc(ve.tensor_tensor(T.nt[:, b:4 * G:4], T.psn[:, 512 * b:512 * b + G], T["dc%d" % t][:, b:4 * G:4], Op.add), "dv")
         wait(ve, "dv")
         inc(quant(cw, G, G + 128, T.nt[:]), "wn")
-        wait(ac, "y")
-        for i in range(2):
-            inc(ac.activation(T.ysb[:, 32 * t + i:32 * t + 32:2], T.psp[:, 32 * i:32 * i + G], Act.Copy), "yc")
+        if t:
+            results(t)
         for q in (ve, ac):
             wait(q, "wn")
         inc(pickc(cn, 0, G, cw, 0, C2, T.fin[:, 0:1]), "cn")
         inc(picks(cn, 0, G, cw, 0, C2, T.fin[:, 0:1]), "cns")
         wait(sy, "id")
-        inc(sy.dma_start(T.ids[0:1, 32 * t:32 * t + 32], T["idt%d" % t][0:G, 0:2]), "out", 16)
-        wait(sy, "yc")
-        inc(sy.dma_start(T.y[:, 32 * t:32 * t + 32], T.ysb[:, 32 * t:32 * t + 32]), "out", 16)
+        inc(sy.dma_start(T.ids[0:1, C2 * t:C2 * t + C2], T["idt%d" % t][0:G, 0:2]), "out", 16)
         if t + 1 < R:
             nxt = "call%d" % (t + 1)
             wait(g, "cn")
@@ -303,13 +334,16 @@ def rank_program(g, core, T, topo):
             to_all((sc(cn, 0, G), sc(nxt, G * r, G * r + G)), "arrc%d" % (t + 1))
             inc(pickc(nxt, G * r, G * r + G, cw, 0, C2, T.fin[:, 0:1]), "own")
             inc(picks(nxt, G * r, G * r + G, cw, 0, C2, T.fin[:, 0:1]), "own")
-            wait(te, "cn", "cns")
+            rest_setup()
+            results(t)
+            wait(te, "cn", "cns", "ke")
             unpack(t + 1)
-    wait(sy, "cn", "cns")
+    wait(sy, "cn")
     inc(sy.dma_start(T.oc[:], cc("cw%d" % R, 0, G)), "out", 16)
+    wait(sy, "cns")
     wait(ac, "cns")
     for k in range(4):
-        q, s = ((sy, "out"), (ac, "outs"))[k % 2 if k else 1]
+        q, s = ((sy, "out"), (ac, "outs"))[k % 2]
         inc(q.dma_start(T.osc[4 * k:4 * k + 4, :], T["cw%ds" % R][32 * k:32 * k + 4, 0:G]), s, 16)
     for name in count:
         if seen.get(name, 0) < count[name]:

from concourse.bass import DstId, RemoteDMATransfer
from concourse.mybir import dt, AluOpType as Op, AxisListType, ActivationFunctionType as Act

N, G, TOK, CAPP, R = 8, 16, 96, 32, 2
C2 = 2 * G
LW = N * C2

_F, _B, _U, _I, _Q, _S = "float32", "bfloat16", "uint16", "int32", "float8_e4m3fn_x4", "uint8"
SCRATCH = {}


def _buf(name, n, d):
    SCRATCH[name] = ("sbuf", [128, n], d)


def _mx(name, n):
    _buf(name + "c", n, _Q)
    _buf(name + "s", n, _S)


for _n, _w in (("cbt", 512), ("xt", 896), ("wt", 512), ("zt", 512), ("ub", 512), ("ab", 2048), ("ob", 512), ("m16", 512),
               ("eb", 2048), ("hb", 544), ("fb", 516), ("nt", 512)):
    _buf(_n, _w, _B)
for _n, _w in (("xq", 224), ("wq", 128), ("uq", 128), ("aq", 512), ("oq", 128), ("eq", 512), ("hq", 136), ("fa", 192),
               ("fo", 192), ("cw0", 144), ("cw1", 144), ("cw2", 16), ("call0", 128), ("call1", 128), ("slot0", 256),
               ("slot1", 256), ("land0", 384), ("land1", 384), ("pick", 144)):
    _mx(_n, _w)
for _n, _w in (("jj", 128), ("zf", 128), ("cm", 128), ("gcol", 1), ("rst", 48), ("rv", 16),
               ("cum", 16), ("lt", 48), ("sc", 48), ("thr", 1), ("mv", 1), ("num", 16), ("numv", 16),
               ("eq1", 16), ("eq2", 16), ("id1", 16), ("id2", 16), ("idr", 2), ("idt0", 2), ("idt1", 2), ("dc0", 64), ("dc1", 64),
               ("ysb", 64)):
    _buf(_n, _w, _F)
for _n, _w in (("v0", 16), ("v1", 16), ("lst0", 16), ("lst1", 16), ("lists0", 16), ("lists1", 16), ("po", 4), ("fin", 2),
               ("own16", 2)):
    _buf(_n, _w, _U)
for _n, _w in (("pi", 1), ("pg", 1), ("xi", 16), ("xa", 16), ("li", 16), ("lf", 16), ("ll", 16), ("idb", 16)):
    _buf(_n, _w, _I)
for _n, _w in (("pss", 512), ("psp", 512), ("psf", 512), ("psn", 2048)):
    SCRATCH[_n] = ("psum", [128, _w], _F)

SEMAPHORES = ["ldc", "ldx", "ldw", "io", "io2", "dv", "z", "zc", "za", "zu", "ze", "kb", "ku", "ka", "ke", "q0", "qx", "qw", "own",
              "arrc0", "arrc1", "arrl0", "arrl1", "arrt0", "arrt1", "sent", "s", "cm", "h", "hq", "pc", "fa", "fo", "fs",
              "l", "v", "pk", "pks", "ol", "pp", "n0", "n1", "n2", "n3", "y", "yc", "wn", "cn", "cns", "dd", "dc", "id", "out", "outs"]


def rank_program(g, core, T, topo):
    r = T.rank_of(core)
    if r is None:
        return
    ve, ac, te, sy = g.vector, g.scalar, g.tensor, g.sync
    count, seen = {}, {}

    def inc(call, name, n=1):
        call.then_inc(T.sem[name], n)
        count[name] = count.get(name, 0) + n

    def wait(queue, *names):
        for name in names:
            queue.wait_ge(T.sem[name], count[name])
            seen[name] = count[name]

    def cc(name, a, b):
        return T[name + "c"][:, a:b].bitcast(dt.uint8)

    def sc(name, a, b):
        return T[name + "s"][:, a:b]

    def quant(name, a, b, tile):
        return ve.quantize_mx(T[name + "c"][:, a:b], T[name + "s"][:, a:b], tile)

    def mm(out, w, wa, x, xa, xb, start=True, stop=True):
        return te.matmul_mx(out, T[w + "c"][:, wa:wa + 128], T[w + "s"][:, wa:wa + 128], T[x + "c"][:, xa:xb],
                            T[x + "s"][:, xa:xb], start, stop)

    def pickc(dst, a, b, src, c, d, offs):
        return ve.tensor_copy(T[dst + "c"][:, a:b].bitcast(dt.uint32), T[src + "c"][:, c:d].bitcast(dt.uint32).indirect(offs))

    def picks(dst, a, b, src, c, d, offs):
        return ac.activation(T[dst + "s"][:, a:b], T[src + "s"][:, c:d].indirect(offs), Act.Copy)

    others = [d for d in range(N) if d != r]
    dest = {}
    for d in others:
        rid, pid = topo.addr(T.cores[d], core)
        dest[d] = DstId(rid=rid, pnc=pid)

    def rest_of(s):
        return [d for d in range(N) if d != s]

    def engines(s):
        return topo.engines(T.cores[s], T.cores[rest_of(s)[0]])

    def deal(s, kind):
        o, e = rest_of(s), engines(s)
        w, h = len(e) // 4, len(e) // 2
        f = e[h:] + e[:h] if kind else e
        return [{o[i]: e[w * i:w * i + w] for i in range(4)}, {o[4]: f[0:w], o[5]: f[w:h], o[6]: f[h:]}]

    def fused(parts, src, dst, sem):
        g.remote_dma_fused([RemoteDMATransfer(dst_ids=[dest[d]], dma_engine_mask=sum(1 << e for e in es), remote_sem=T.sem[sem],
                                              srcs=[src(d)], dsts=[dst]) for d, es in parts.items()], local_sem=T.sem.sent)
        count["sent"] = count.get("sent", 0) + sum(len(es) for es in parts.values())

    def to_all(view, sem):
        es = engines(r)
        g.remote_dma_fused([RemoteDMATransfer(dst_ids=[dest[d] for d in others], dma_engine_mask=sum(1 << e for e in es),
                                              remote_sem=T.sem[sem], srcs=[view[0]], dsts=[view[1]] * len(others))],
                           local_sem=T.sem.sent)
        count["sent"] = count.get("sent", 0) + len(es)

    arrive_c = sum(2 * len(engines(s)) for s in others)
    arrive_t = sum(len(p[r]) for s in others for kind in range(2) for p in deal(s, kind) if r in p)

    inc(sy.dma_start(T.cbt[:, 0:4 * G], T.cb[:]), "ldc", 16)
    inc(ac.dma_start(T.xt[:, 0:768], T.x[:]), "ldx", 16)
    inc(sy.dma_start(T.wt[:], T.w[:]), "ldw", 16)
    inc(g.iota(T.pi[:], [[0, 1]], 0, 1), "io")
    inc(g.iota(T.jj[:], [[1, 128]], 0, -1, allow_small_or_imprecise_dtypes=True), "io")
    inc(g.iota(T.m16[:], [[0, 8], [1, 16], [-1, 4]], 0, 0, allow_small_or_imprecise_dtypes=True), "io")
    inc(ve.memset(T.zt[:], 0.0), "z")
    inc(ve.memset(T.cbt[:, 4 * G:512], 0.0), "zc")
    inc(ve.memset(T.xt[:, 768:896], 0.0), "za")
    inc(ve.memset(T.hb[:], 0.0), "za")
    inc(ve.memset(T.fb[:], 0.0), "za")
    inc(ve.memset(T.zf[:], 0.0), "za")
    wait(ve, "z")
    inc(quant("fa", 64, 192, T.zt[:]), "ka")
    inc(quant("fo", 64, 192, T.zt[:]), "ka")
    wait(ac, "z")
    inc(ac.activation(T.ub[:], T.zt[:], Act.Copy), "zu")
    inc(ac.activation(T.ob[:], T.zt[:], Act.Copy), "zu")
    wait(ve, "zc", "ldc")
    inc(quant("cw0", 0, 128, T.cbt[:]), "q0")
    wait(g, "q0")
    to_all((cc("cw0", 0, G), cc("call0", G * r, G * r + G)), "arrc0")
    to_all((sc("cw0", 0, G), sc("call0", G * r, G * r + G)), "arrc0")
    inc(g.iota(T.idb[:], [[TOK, N], [0, 2]], 1, 0), "io2")
    wait(ve, "za", "ldx")
    inc(quant("xq", 0, 224, T.xt[:]), "qx")
    wait(ve, "io")
    inc(ve.tensor_scalar(T.pg[:], T.pi[:], G - 1, None, Op.bitwise_and), "dv")
    inc(ve.memset(T.hb[0:TOK, 0:1], 1.0), "za")
    inc(ve.memset(T.hb[0:TOK, 512:513], 1.0), "za")
    wait(ve, "dv", "zu")
    inc(ve.tensor_copy(T.gcol[:], T.pg[:]), "dv")
    inc(ve.tensor_copy(T.own16[:, 0:1], T.pg[:]), "dv")
    inc(ve.tensor_scalar(T.ub[:, 0:512:4], T.jj[:], 0.0, None, Op.is_ge), "kb")
    inc(ve.tensor_scalar(T.ub[:, 1:512:4], T.jj[:], 0.0, -1.0, Op.is_ge, Op.mult), "kb")
    inc(ve.memset(T.ob[:, 0:512:4], 128.0), "kb")
    wait(ve, "dv", "q0")
    wait(ac, "dv", "q0")
    inc(pickc("call0", G * r, G * r + G, "cw0", 0, G, T.own16[:, 0:1]), "own")
    inc(picks("call0", G * r, G * r + G, "cw0", 0, G, T.own16[:, 0:1]), "own")
    for b in range(4):
        inc(ac.activation(T.eb[:, 512 * b:512 * b + 512], T.zt[:], Act.Copy), "ze")
    inc(ac.activation(T.nt[:], T.zt[:], Act.Copy), "ze")
    wait(ve, "kb")
    inc(quant("uq", 0, 128, T.ub[:]), "ku")
    for q in range(4):
        inc(ve.tensor_scalar(T.ab[:, 512 * q:512 * q + 512], T.m16[:], 4.0 * q, None, Op.is_equal), "kb")
    inc(quant("oq", 0, 128, T.ob[:]), "ka")
    wait(ve, "kb")
    inc(quant("aq", 0, 512, T.ab[:]), "ka")

    def unpack(t):
        for b in range(4):
            inc(mm(T.psn[:, 512 * b:512 * b + 128], "eq", 128 * b, "cw%d" % t, 0, 128), "dd")
        wait(ac, "dd")
        for b in range(4):
            inc(ac.activation(T["dc%d" % t][:, b:4 * G:4], T.psn[:, 512 * b:512 * b + G], Act.Copy, scale=2.0), "dc")

    def late_setup():
        wait(ve, "ze")
        for b in range(4):
            inc(ve.tensor_scalar(T.eb[:, 512 * b + b:512 * b + 512:4], T.jj[:], 0.0, 0.25, Op.is_equal, Op.mult), "dv")
        inc(ve.memset(T.rst[:], 1.0), "dv")
        wait(ve, "dv")
        inc(ve.memset(T.rst[:, 0:48:16], 0.0), "dv")
        inc(quant("eq", 0, 512, T.eb[:]), "ke")
        inc(quant("pick", 16, 144, T.zt[:]), "ke")
        inc(quant("land0", LW, LW + 128, T.zt[:]), "ke")
        wait(te, "q0", "ke")
        unpack(0)

    def rest_setup():
        inc(quant("cw1", G, G + 128, T.zt[:]), "ke")
        wait(ve, "ldw")
        inc(quant("wq", 0, 128, T.wt[:]), "qw")
        inc(quant("land1", LW, LW + 128, T.zt[:]), "ke")

    def results(t):
        wait(te, "qw")
        inc(mm(T.psp[:, 0:128], "wq", 0, "pick", 0, 128), "y")
        wait(ac, "y")
        for i in range(2):
            inc(ac.activation(T.ysb[:, C2 * t + i:C2 * t + C2:2], T.psp[:, 32 * i:32 * i + G], Act.Copy), "yc")
        wait(sy, "yc")
        inc(sy.dma_start(T.y[:, C2 * t:C2 * t + C2], T.ysb[:, C2 * t:C2 * t + C2]), "out", 16)

    for t in range(R):
        call_, cw, cn = "call%d" % t, "cw%d" % t, "cw%d" % (t + 1)
        slot, land, v, lst, lists = "slot%d" % t, "land%d" % t, T["v%d" % t], T["lst%d" % t], T["lists%d" % t]
        x0 = TOK * t
        if t == 0:
            wait(te, "qx", "ku")
        wait(te, "own")
        te.wait_ge(T.sem["arrc%d" % t], arrive_c)
        inc(mm(T.pss[:, 0:128], "xq", x0, call_, 0, 128), "s")
        wait(ve, "za", "s")
        inc(ve.tensor_tensor_scan(T.cm[:], T.pss[:, 0:128], T.zf[:], -1e29, Op.max, Op.add), "cm")
        wait(ve, "cm")
        wait(ac, "za", "cm")
        best = T.cm[0:TOK, 127:128]
        inc(ve.tensor_scalar(T.hb[0:TOK, 4:512:4], T.cm[0:TOK, 0:127], best, None, Op.is_lt), "h")
        inc(ac.activation(T.hb[0:TOK, 1:512:4], T.cm[0:TOK, :], Act.Sign, bias=best, scale=-1.0), "h")
        inc(ve.tensor_scalar(T.hb[0:TOK, 516:544:4], T.cm[0:TOK, 15:127:16], best, None, Op.is_lt), "h")
        inc(ac.activation(T.hb[0:TOK, 513:544:4], T.cm[0:TOK, 15:128:16], Act.Sign, bias=best, scale=-1.0), "h")
        wait(ve, "h")
        inc(quant("hq", 0, 136, T.hb[:]), "hq")
        if t:
            wait(te, "yc")
        wait(te, "hq")
        inc(mm(T.psp[:, 0:136], "uq", 0, "hq", 0, 136), "pc")
        if t == 0:
            wait(te, "ka")
        wait(ve, "pc")
        inc(ve.tensor_scalar(T.fb[0:TOK, 0:128], T.psp[0:TOK, 0:128], 1.0, None, Op.is_lt), "dv")
        inc(ve.tensor_scalar(T.fb[0:TOK, 128:256], T.psp[0:TOK, 0:128], 2.0, None, Op.is_lt), "dv")
        for i in range(2):
            inc(ve.tensor_scalar(T.fb[0:TOK, 256 + 128 * i:384 + 128 * i:16], T.psp[0:TOK, 128:136], float(CAPP + 1), None, Op.is_lt), "dv")
        wait(ve, "dv")
        inc(quant("fa", 0, 128, T.fb[:, 0:512]), "fa")
        inc(quant("fo", 0, 128, T.fb[:, 4:516]), "fo")
        wait(te, "fa")
        ps = T.psf[:, 0:128]
        mm(ps, "aq", 0, "fa", 0, 128, True, False)
        mm(ps, "aq", 256, "fa", 2, 130, False, False)
        mm(ps, "oq", 0, "fa", 64, 192, False, False)
        wait(te, "fo")
        mm(ps, "aq", 128, "fo", 0, 128, False, False)
        inc(mm(ps, "aq", 384, "fo", 2, 130, False, True), "fs")
        wait(ve, "fs")
        for i in range(2):
            inc(ve.tensor_copy(lst[:, i:16:2], T.psf[:, 32 * i:32 * i + 32:4]), "l")
        inc(ve.tensor_copy(T.xi[:], T.psf[:, 0:64:4]), "dv")
        wait(g, "l")
        fused({d: [engines(r)[i]] for i, d in enumerate(others)}, lambda d: lst[:, 2 * d:2 * d + 2], lists[:, 2 * r:2 * r + 2], "arrl%d" % t)
        wait(ve, "dv")
        inc(ve.tensor_scalar(T.xa[:], T.xi[:], 127, None, Op.bitwise_and), "dv")
        wait(ve, "dv")
        for i in range(2):
            inc(ve.tensor_copy(v[:, i:16:2], T.xa[:, 8 * i:8 * i + 8]), "v")
        wait(ve, "v")
        wait(ac, "v")
        inc(pickc(slot, 0, LW, "xq", x0, 224, v[:]), "pk")
        inc(picks(slot, 0, LW, "xq", x0, 224, v[:]), "pks")
        wait(g, "pk")
        for part in deal(r, 0):
            fused(part, lambda d: cc(slot, C2 * d, C2 * d + C2), cc(land, C2 * r, C2 * r + C2), "arrt%d" % t)
        wait(g, "pks")
        for part in deal(r, 1):
            fused(part, lambda d: sc(slot, C2 * d, C2 * d + C2), sc(land, C2 * r, C2 * r + C2), "arrt%d" % t)
        inc(pickc(land, C2 * r, C2 * r + C2, "xq", x0, 224, v[:, 2 * r:2 * r + 2]), "ol")
        inc(picks(land, C2 * r, C2 * r + C2, "xq", x0, 224, v[:, 2 * r:2 * r + 2]), "ol")
        if t == 0:
            late_setup()
        def take(src, a, b):
            if a < b:
                inc(ve.tensor_copy(T.li[:, a:b], src[:, a:b]), "dv")
        wait(ve, "l")
        take(lst, 2 * r, 2 * r + 2)
        ve.wait_ge(T.sem["arrl%d" % t], len(others))
        take(lists, 0, 2 * r)
        take(lists, 2 * r + 2, 16)
        wait(ve, "dv", "io2")
        inc(ve.tensor_scalar(T.lf[:], T.li[:], 127, None, Op.bitwise_and), "dv")
        inc(ve.tensor_scalar(T.ll[:], T.li[:], 7, None, Op.logical_shift_right), "dv")
        wait(ve, "dv")
        inc(ve.tensor_tensor(T.rv[:], T.lf[:], T.ll[:], Op.is_lt), "dv")
        inc(ve.tensor_tensor(T.num[:], T.lf[:], T.idb[:], Op.add), "dv")
        wait(ve, "dv")
        inc(ve.tensor_tensor_scan(T.cum[:], T.rv[:], T.zf[:, 0:16], 0.0, Op.add, Op.add), "dv")
        wait(ve, "dv")
        inc(ve.tensor_scalar(T.thr[:], T.cum[:, 15:16], 2.0, None, Op.min), "dv")
        inc(ve.tensor_scalar(T.mv[:], T.cum[:, 15:16], 1.0, float(G), Op.min, Op.mult), "dv")
        inc(ve.tensor_scalar(T.lt[:, 0:16], T.cum[:], 1.0, None, Op.is_lt), "dv")
        inc(ve.tensor_scalar(T.lt[:, 32:48], T.cum[:], 2.0, None, Op.is_lt), "dv")
        wait(ve, "dv")
        inc(ve.tensor_scalar(T.lt[:, 16:32], T.cum[:], T.thr[:], None, Op.is_lt), "dv")
        inc(ve.tensor_scalar(T.fin[:, 0:1], T.mv[:], T.gcol[:], None, Op.add), "dv")
        wait(ve, "dv")
        inc(ve.tensor_tensor_scan(T.sc[:], T.rst[:], T.lt[:], 0.0, Op.mult, Op.add), "dv")
        inc(ve.tensor_tensor(T.numv[:], T.num[:], T.rv[:], Op.mult), "dv")
        wait(ve, "dv")
        inc(ve.tensor_scalar(T.po[:, 0:3], T.sc[:, 15:48:16], float(G), T.gcol[:], Op.mult, Op.add), "dv")
        inc(ve.tensor_scalar(T.eq1[:], T.cum[:], 1.0, None, Op.is_equal), "dv")
        inc(ve.tensor_scalar(T.eq2[:], T.cum[:], 2.0, None, Op.is_equal), "dv")
        for q in (ve, ac):
            wait(q, "dv", "ol", "ke")
            q.wait_ge(T.sem["arrt%d" % t], arrive_t)
        wait(te, "dc")
        inc(pickc("pick", 0, 48, land, 0, LW + G, T.po[:, 0:3]), "pp")
        inc(picks("pick", 0, 48, land, 0, LW + G, T.po[:, 0:3]), "pp")
        wait(te, "pp")
        for b in range(4):
            bank = T.psn[:, 512 * b:512 * b + 128]
            mm(bank, "eq", 128 * b, "pick", 0, 128, True, False)
            inc(mm(bank, "eq", 128 * b, "pick", 16, 144, False, True), "n%d" % b)
        inc(ve.tensor_tensor(T.id1[:], T.numv[:], T.eq1[:], Op.mult), "dv")
        inc(ve.tensor_tensor(T.id2[:], T.numv[:], T.eq2[:], Op.mult), "dv")
        wait(ve, "dv")
        inc(ve.tensor_reduce(T.idr[:, 0:1], T.id1[:], AxisListType.X, Op.add), "dv")
        inc(ve.tensor_reduce(T.idr[:, 1:2], T.id2[:], AxisListType.X, Op.add), "dv")
        wait(ve, "dv", "dc")
        inc(ve.tensor_scalar(T["idt%d" % t][:], T.idr[:], -1.0, None, Op.add), "id")
        for b in range(4):
            wait(ve, "n%d" % b)
            inc(ve.tensor_tensor(T.nt[:, b:4 * G:4], T.psn[:, 512 * b:512 * b + G], T["dc%d" % t][:, b:4 * G:4], Op.add), "dv")
        wait(ve, "dv")
        inc(quant(cw, G, G + 128, T.nt[:]), "wn")
        if t:
            results(t)
        for q in (ve, ac):
            wait(q, "wn")
        inc(pickc(cn, 0, G, cw, 0, C2, T.fin[:, 0:1]), "cn")
        inc(picks(cn, 0, G, cw, 0, C2, T.fin[:, 0:1]), "cns")
        wait(sy, "id")
        inc(sy.dma_start(T.ids[0:1, C2 * t:C2 * t + C2], T["idt%d" % t][0:G, 0:2]), "out", 16)
        if t + 1 < R:
            nxt = "call%d" % (t + 1)
            wait(g, "cn")
            to_all((cc(cn, 0, G), cc(nxt, G * r, G * r + G)), "arrc%d" % (t + 1))
            wait(g, "cns")
            to_all((sc(cn, 0, G), sc(nxt, G * r, G * r + G)), "arrc%d" % (t + 1))
            inc(pickc(nxt, G * r, G * r + G, cw, 0, C2, T.fin[:, 0:1]), "own")
            inc(picks(nxt, G * r, G * r + G, cw, 0, C2, T.fin[:, 0:1]), "own")
            rest_setup()
            results(t)
            wait(te, "cn", "cns", "ke")
            unpack(t + 1)
    wait(sy, "cn")
    inc(sy.dma_start(T.oc[:], cc("cw%d" % R, 0, G)), "out", 16)
    wait(sy, "cns")
    wait(ac, "cns")
    for k in range(4):
        q, s = ((sy, "out"), (ac, "outs"))[k % 2]
        inc(q.dma_start(T.osc[4 * k:4 * k + 4, :], T["cw%ds" % R][32 * k:32 * k + 4, 0:G]), s, 16)
    for name in count:
        if seen.get(name, 0) < count[name]:
            wait(g, name)
